import numpy as np
import ml_dtypes


def mxq(x, axis, fmt="e4m3"):
    dtype, down = {"e4m3": (ml_dtypes.float8_e4m3fn, 7), "e5m2": (ml_dtypes.float8_e5m2, 14)}[fmt]
    v = np.moveaxis(np.asarray(x, np.float32).astype(ml_dtypes.bfloat16).astype(np.float64), axis, -1)
    blocks = v.reshape(v.shape[:-1] + (-1, 32))
    amax = np.abs(blocks).max(-1, keepdims=True)
    byte = np.maximum(np.where(amax > 0, np.frexp(amax)[1] - 1 + 127, 0) - down, 1)
    scale = np.exp2(byte - 127.0)
    codes = (blocks / scale).astype(np.float32).astype(dtype).astype(np.float64)
    return np.moveaxis((codes * scale).reshape(v.shape), -1, axis)


WIDE = False


def mx_kscale(k):
    if not WIDE:
        return np.ones(k)
    levels = np.array([10, -10, 5, -5, 0])
    if k % 512:
        return np.exp2(np.random.permutation(np.resize(levels, k // 32))).repeat(32)
    a = np.empty((k // 512, 16))
    for p in range(k // 512):
        a[p, :8] = np.random.permutation(np.resize(levels, 8))
        for g in range(8):
            far = levels[np.abs(levels - a[p, g]) >= 10]
            a[p, g + 8] = far[np.random.randint(len(far))]
    return np.exp2(a.ravel()).repeat(32)


BF16 = ml_dtypes.bfloat16


def bf(x):
    return np.asarray(x, np.float32).astype(BF16)


def f64(x):
    return np.asarray(x).astype(np.float64)


E2M1 = np.array([0.0, 0.5, 1.0, 1.5, 2.0, 3.0, 4.0, 6.0, -0.0, -0.5, -1.0, -1.5, -2.0, -3.0, -4.0, -6.0])


def pack_weight(w, fmt):
    k, n = w.shape
    w = f64(bf(w)).reshape(k // 32, 32, n)
    amax = np.abs(w).max(1)
    if fmt == "e4m3":
        byte = np.frexp(amax)[1] - 1 + 127 - 7
    else:
        mant, ex = np.frexp(amax / 6.0)
        byte = np.where(mant > 0.5, ex, ex - 1) + 127
    byte = np.clip(np.where(amax > 0, byte, 1), 1, 254)
    scaled = (w * np.exp2(127.0 - byte)[:, None, :]).reshape(k, n).astype(np.float32)
    by_word = np.ascontiguousarray(scaled.reshape(k // 512, 128, 4, n).transpose(0, 1, 3, 2))
    if fmt == "e4m3":
        words = by_word.astype(ml_dtypes.float8_e4m3fn).view(np.uint8)
    else:
        c = by_word.astype(ml_dtypes.float4_e2m1fn).view(np.uint8) & 0xF
        words = c[..., 0::2] | (c[..., 1::2] << 4)
    return np.ascontiguousarray(words), np.ascontiguousarray(byte.astype(np.uint8).reshape(k // 512, 16, n))


def unpack_weight(words, scales, fmt):
    g, p, n, _ = words.shape
    if fmt == "e4m3":
        vals = np.ascontiguousarray(words).view(ml_dtypes.float8_e4m3fn).astype(np.float64)
    else:
        nib = np.empty((g, p, n, 4), np.uint8)
        nib[..., 0::2] = words & 0xF
        nib[..., 1::2] = words >> 4
        vals = E2M1[nib]
    vals = vals * np.repeat(np.exp2(scales.astype(np.float64) - 127.0), 8, axis=1)[..., None]
    return vals.transpose(0, 1, 3, 2).reshape(g * 512, n)
def pack4(w):
    words, scales = pack_weight(w, "e2m1")
    return words.reshape(words.shape[0], 128, -1), scales


def unpack4(words, scales):
    return unpack_weight(words.reshape(words.shape[0], 128, -1, 2), scales, "e2m1")


T, F, P, D = 2048, 1536, 1024, 1024


def setup_inputs():
    s = mx_kscale(F)
    t = mx_kscale(P)
    spec = np.random.standard_normal((F, T)) * s[:, None]
    comb = np.random.standard_normal((F, P)) / np.sqrt(F) / s[:, None]
    table = np.random.standard_normal((P, D)) / np.sqrt(P) / t[:, None]
    spec_words, spec_scales = pack4(spec)
    comb_words, comb_scales = pack4(comb)
    table_words, table_scales = pack_weight(table, "e4m3")
    return {"spec_words": spec_words, "spec_scales": spec_scales,
            "comb_words": comb_words, "comb_scales": comb_scales,
            "prior": bf(np.exp(0.3 * np.random.standard_normal(P)) * t),
            "table_words": table_words, "table_scales": table_scales,
            "voicing": bf(np.random.uniform(0.2, 1.0, T))}


def reference(spec_words, spec_scales, comb_words, comb_scales, prior, table_words, table_scales, voicing):
    spec = unpack4(spec_words, spec_scales)
    comb = unpack4(comb_words, comb_scales)
    table = unpack_weight(table_words, table_scales, "e4m3")
    z = spec.T @ comb
    sal = np.exp(z) * f64(prior)
    y = mxq(sal, 1, "e4m3") @ table
    return y * f64(voicing)[:, None]

from contextlib import ExitStack

import concourse.mybir as mybir

T, F, PITCH, D = 2048, 1536, 1024, 1024
FLOPS = 2 * T * F * PITCH + 2 * T * PITCH * D

F32 = mybir.dt.float32
BF16 = mybir.dt.bfloat16
I32 = mybir.dt.int32
U32 = mybir.dt.uint32
U8 = mybir.dt.uint8
FP4X4 = mybir.dt.float4_e2m1fn_x4
FP8X4 = mybir.dt.float8_e4m3fn_x4
ACT = mybir.ActivationFunctionType
ALU = mybir.AluOpType

P = 128
PACK = 4
K_PASS = P * PACK
N = 512
BIN_PASSES = F // K_PASS
PITCH_GROUPS = PITCH // K_PASS
CHUNKS = T // N
TILES = N // P
HALVES = D // N
BANKS = 8
EXP_BUFS = 8
SAL_BUFS = 3
WORD_BUFS = 8
OUT_BUFS = 6
LAG = 3


def tile_pitch_salience_embed_s4_kernel(
    tc, spec_words, spec_scales, comb_words, comb_scales, prior, table_words, table_scales, voicing, out
):
    nc = tc.nc

    with ExitStack() as ctx:
        sbuf = ctx.enter_context(tc.tile_pool(name="sbuf", bufs=1))
        psum = ctx.enter_context(tc.psum_pool(name="psum", bufs=1))
        ctx.enter_context(tc.manual_schedule())

        def new_plane(name, passes, width):
            plane = sbuf.tile([P, passes, width], U8, name=name, align_bytes=64)
            nc.vector.memset(plane[:].rearrange("p g n -> p (g n)").bitcast(I32), 0)
            return plane

        def load_plane(plane, scales, cols):
            for q in range(4):
                nc.sync.dma_start(
                    out=plane[32 * q : 32 * q + 4, :, :].bitcast(I32),
                    in_=scales[:, 4 * q : 4 * q + 4, cols].rearrange("g r n -> r g n").bitcast(I32),
                )

        def load_words(name, words, passes, cols):
            width = cols.stop - cols.start
            tile = sbuf.tile([P, passes.stop - passes.start, width], U8, name=name, align_bytes=64)
            nc.sync.dma_start(
                out=tile[:].bitcast(I32), in_=words[passes, :, cols].rearrange("g p n -> p g n").bitcast(I32)
            )
            return [tile[:, g, :] for g in range(passes.stop - passes.start)]

        first, later, every = slice(0, 1), slice(1, BIN_PASSES), slice(0, BIN_PASSES)

        comb_plane = [new_plane("comb_plane0", BIN_PASSES, K_PASS)]
        spec_plane_first = new_plane("spec_plane_first", BIN_PASSES, N)
        comb_plane.append(new_plane("comb_plane1", BIN_PASSES, K_PASS))
        spec_plane_later = new_plane("spec_plane_later", BIN_PASSES, T - N)
        table_plane = new_plane("table_plane", PITCH_GROUPS, D)

        comb_raw = [load_words("comb_first", comb_words, first, slice(0, 2 * K_PASS))]
        load_plane(comb_plane[0], comb_scales, slice(0, K_PASS))
        spec = [load_words("spec_first", spec_words, first, slice(0, 2 * N))]
        load_plane(spec_plane_first, spec_scales, slice(0, N))
        comb_raw[0].extend(load_words("comb_later", comb_words, later, slice(0, 2 * K_PASS)))
        spec[0].extend(load_words("spec_later", spec_words, later, slice(0, 2 * N)))
        load_plane(comb_plane[1], comb_scales, slice(K_PASS, 2 * K_PASS))
        comb_raw.append(load_words("comb1", comb_words, every, slice(2 * K_PASS, 4 * K_PASS)))
        prior_bf = sbuf.tile([P, PITCH_GROUPS, PACK], BF16, name="prior_bf")
        nc.sync.dma_start(out=prior_bf[:], in_=prior.rearrange("(g p t) -> p g t", p=P, t=PACK))
        load_plane(spec_plane_later, spec_scales, slice(N, T))
        spec.append(load_words("spec1", spec_words, every, slice(2 * N, 4 * N)))
        load_plane(table_plane, table_scales, slice(0, D))
        table = load_words(
            "table", table_words.rearrange("g p n t -> g p (n t)"), slice(0, PITCH_GROUPS), slice(0, PACK * D)
        )
        voicing_bf = sbuf.tile([P, CHUNKS, TILES], BF16, name="voicing_bf")
        nc.sync.dma_start(out=voicing_bf[:], in_=voicing.rearrange("(c p j) -> p c j", p=P, j=TILES))
        for c in range(2, CHUNKS):
            spec.append(load_words("spec%d" % c, spec_words, every, slice(2 * N * c, 2 * N * (c + 1))))

        def spec_scale(c, g):
            if c == 0:
                return spec_plane_first[:, g, :]
            return spec_plane_later[:, g, N * (c - 1) : N * c]

        comb = {}

        def sort_comb(grp, g):
            codes = sbuf.tile([P, PACK, 2 * P], U8, name="comb_codes%d_%d" % (grp, g), align_bytes=64)
            scales = sbuf.tile([P, PACK, P], U8, name="comb_scales%d_%d" % (grp, g), align_bytes=64)
            nc.vector.tensor_copy(
                out=codes[:].rearrange("p t (m b) -> p t m b", b=2),
                in_=comb_raw[grp][g].rearrange("p (m t b) -> p t m b", t=PACK, b=2),
            )
            nc.vector.tensor_copy(out=scales[:], in_=comb_plane[grp][:, g, :].rearrange("p (m t) -> p t m", t=PACK))
            comb[grp, g] = (codes, scales)

        used_banks = []

        def new_bank():
            bank = psum.tile([P, N], F32, name="bank%d" % (len(used_banks) % BANKS))
            used_banks.append(bank)
            return bank

        def match_pass(bank, c, grp, t, g):
            codes, scales = comb[grp, g]
            nc.tensor.matmul_mx(
                out=bank[:],
                lhsT=codes[:, t, :].bitcast(FP4X4),
                lhsT_scale=scales[:, t, :],
                rhs=spec[c][g].bitcast(FP4X4),
                rhs_scale=spec_scale(c, g),
                start=(g == 0),
                stop=(g == BIN_PASSES - 1),
            )

        def exp_of(bank, step, t):
            e = sbuf.tile([P, TILES, P], F32, name="exp%d" % ((PACK * step + t) % EXP_BUFS))
            nc.scalar.activation(out=e[:], in_=bank[:].rearrange("p (m j) -> p j m", j=TILES), func=ACT.Exp)
            return e

        def times_prior(sal, e, grp, t, tiles):
            nc.vector.tensor_scalar(
                out=sal[:, tiles, t, :], in0=e[:, tiles, :], scalar1=prior_f[:, grp, t : t + 1], scalar2=None, op0=ALU.mult
            )

        salience = {}

        def quantise_group(sal, step):
            c, grp = divmod(step, PITCH_GROUPS)
            words = []

            def interleave(j):
                w = sbuf.tile([P, P, PACK], BF16, name="words%d" % ((TILES * step + j) % WORD_BUFS), align_bytes=64)
                nc.vector.tensor_copy(
                    out=w[:].rearrange("p (a i) t -> p a t i", i=4),
                    in_=sal[:, j, :, :].rearrange("p t (a i) -> p a t i", i=4),
                )
                words.append(w)

            def quantise(j):
                codes = sbuf.tile([P, P], U32, name="sal_codes%d_%d" % (step, j), align_bytes=64)
                scales = sbuf.tile([P, P], U8, name="sal_scales%d_%d" % (step, j), align_bytes=64)
                nc.vector.quantize_mx(
                    out=codes[:].bitcast(FP8X4), scales=scales[:], in_=words[j][:].rearrange("p m t -> p (m t)")
                )
                salience[c, grp, j] = (codes, scales)

            interleave(0)
            for j in range(1, TILES):
                interleave(j)
                quantise(j - 1)
            quantise(TILES - 1)

        out_rows = out.rearrange("(c p j) d -> c j p d", p=P, j=TILES)
        staged = {}

        def embed_bank(i, on_vector):
            tile_no, h = divmod(i, HALVES)
            c, j = divmod(tile_no, TILES)
            cols = slice(N * h, N * (h + 1))
            bank = new_bank()
            for grp in range(PITCH_GROUPS):
                codes, scales = salience[c, grp, j]
                nc.tensor.matmul_mx(
                    out=bank[:],
                    lhsT=codes[:].bitcast(FP8X4),
                    lhsT_scale=scales[:],
                    rhs=table[grp][:, PACK * N * h : PACK * N * (h + 1)].bitcast(FP8X4),
                    rhs_scale=table_plane[:, grp, cols],
                    start=(grp == 0),
                    stop=(grp == PITCH_GROUPS - 1),
                )
            if h == 0:
                staged[tile_no] = sbuf.tile([P, D], F32, name="staged%d" % (tile_no % OUT_BUFS))
            rows = staged[tile_no]
            gain = voicing_f[:, c, j : j + 1]
            if on_vector:
                nc.vector.tensor_scalar(out=rows[:, cols], in0=bank[:], scalar1=gain, scalar2=None, op0=ALU.mult)
            else:
                nc.scalar.activation(out=rows[:, cols], in_=bank[:], func=ACT.Copy, scale=gain)
            if tile_no == CHUNKS * TILES - 1:
                nc.sync.dma_start(out=out_rows[c, j][:, cols], in_=rows[:, cols])
            elif h == HALVES - 1:
                nc.sync.dma_start(out=out_rows[c, j], in_=rows[:])

        steps = CHUNKS * PITCH_GROUPS

        for g in range(BIN_PASSES):
            sort_comb(0, g)
        first_banks = [new_bank() for t in range(PACK)]
        for g in range(BIN_PASSES):
            for t in range(PACK):
                match_pass(first_banks[t], 0, 0, t, g)
        for g in range(BIN_PASSES):
            sort_comb(1, g)
        prior_f = sbuf.tile([P, PITCH_GROUPS, PACK], F32, name="prior_f")
        nc.vector.tensor_copy(out=prior_f[:], in_=prior_bf[:])

        for step in range(steps):
            c, grp = divmod(step, PITCH_GROUPS)
            sal = sbuf.tile([P, TILES, PACK, P], BF16, name="sal%d" % (step % SAL_BUFS))
            if step == LAG:
                voicing_f = sbuf.tile([P, CHUNKS, TILES], F32, name="voicing_f")
                nc.vector.tensor_copy(out=voicing_f[:], in_=voicing_bf[:])
            for t in range(PACK):
                if step == 0:
                    bank = first_banks[t]
                else:
                    bank = new_bank()
                    for g in range(BIN_PASSES):
                        match_pass(bank, c, grp, t, g)
                e = exp_of(bank, step, t)
                if step >= LAG:
                    embed_bank(PACK * (step - LAG) + t, on_vector=(t == 1))
                if t < PACK - 1:
                    times_prior(sal, e, grp, t, slice(0, TILES))
                else:
                    times_prior(sal, e, grp, t, slice(0, TILES // 2))
                    times_prior(sal, e, grp, t, slice(TILES // 2, TILES))
            quantise_group(sal, step)

        tail = PACK * (steps - LAG)
        for i in range(tail, CHUNKS * TILES * HALVES):
            embed_bank(i, on_vector=(i >= tail + PACK and i % 2 == 0))
